import numpy as np, ml_dtypes
CORES = [10,34,74,98]
N = 4
BF = ml_dtypes.bfloat16
def f(rng, *shape):
    return (rng.standard_normal(shape, dtype=np.float32) * np.exp2(rng.integers(-2, 3, shape[:-1] + (1,)))).astype(BF)
def wide(rng, *shape):
    v = f(rng, *shape).astype(np.float32); k = shape[:-2] + (1, shape[-1])
    return (v * np.exp2(rng.integers(-6, 7, k)) * (rng.random(k) > 0.0625)).astype(BF)
P, NT, W, D = 2048, 256, 2048, 32
def order(g):
    return range(N)
def places(ln):
    n = np.asarray(ln).reshape(-1, NT).astype(np.int64) + 1; m = len(n)
    t = np.repeat(np.tile(np.arange(NT), m), n.reshape(-1)).reshape(m, P)
    last = np.zeros((m, P), bool); last[np.arange(m)[:, None], np.add.accumulate(n, 1) - 1] = True
    return t, last
def steps(ln, ds):
    t, last = places(ln); m = len(t); src = np.arange(P) - np.take_along_axis(np.asarray(ds).reshape(m, NT).astype(np.int64), t, 1)
    e = np.zeros((m, P), np.int64); row = np.arange(m)
    for i in range(P):
        j = src[:, i]; e[:, i] = np.where(last[:, i], 0, 1 + np.where(j >= 0, e[row, np.maximum(j, 0)], 0))
    return e
def lengths(rng, at, big):
    n = np.zeros((N, 8, NT), np.int64)
    for r in range(N):
        for g in range(8):
            b = int(big[r, g]); rest = P - NT - b
            v = np.minimum(rng.multinomial(rest, rng.dirichlet(np.where(rng.random(NT - 1) < 0.25, 0.001, 1.0))), D)
            v = v + rng.multivariate_hypergeometric(D - v, rest - int(np.sum(v)))
            n[r, g] = np.insert(v, int(at[r, g]), b)
    return n
def starts(n):
    return np.add.accumulate(n + 1, 2) - n - 1
def distances(rng, n):
    s = starts(n); k = rng.integers(0, 4, n.shape)
    over = rng.integers(np.minimum(s, W - 1) + 1, W + 1)
    return np.where(k == 0, rng.integers(1, 9, n.shape), np.where(k == 3, over, rng.integers(1, W + 1, n.shape)))
def inside(rng, n, d, share):
    s = starts(n); d = np.array(d)
    for g in range(8):
        q = order(g)[0]; m = (d[q, g] > s[q, g]) & (s[q, g] > 0) & (rng.random(NT) < share)
        d[q, g] = np.where(m, rng.integers(1, np.maximum(s[q, g], 1) + 1), d[q, g])
    return d
def fit(n, d):
    d = np.array(d)
    for r in range(N):
        for g in range(8):
            e = []
            for t, (c, k) in enumerate(zip(n[r, g].tolist(), d[r, g].tolist())):
                s = len(e)
                for i in range(s, s + c): e.append(1 + (e[i - k] if i >= k else 0))
                if max(e[s:], default=0) > D:
                    d[r, g, t] = 1; e[s:] = range(1, c + 1)
                e.append(0)
    return d
def pack(rng, n, d):
    return {"ln": n.astype(np.int32), "ds": d.astype(np.int32), "le": f(rng, N, 128, NT)}
def setup_inputs(rng):
    n = lengths(rng, rng.integers(0, NT, (N, 8)), rng.integers(1, D + 1, (N, 8)))
    return pack(rng, n, fit(n, inside(rng, n, distances(rng, n), 0.75)))
def setup_inputs_deep(rng):
    at = np.where(rng.random((N, 8)) < 0.25, rng.choice(np.array([0, NT - 1]), (N, 8)), rng.integers(0, NT, (N, 8)))
    n = lengths(rng, at, np.full((N, 8), D)); d = np.where(rng.random(n.shape) < 0.5, rng.integers(1, 4, n.shape), distances(rng, n))
    d = inside(rng, n, d, 0.75); np.put_along_axis(d, at[:, :, None], 1, 2)
    return pack(rng, n, fit(n, d))
def setup_inputs_hops(rng):
    n = lengths(rng, rng.integers(0, NT, (N, 8)), rng.integers(1, D + 1, (N, 8)))
    return pack(rng, n, fit(n, inside(rng, n, rng.integers(W - 8, W + 1, n.shape), 1.0)))
def setup_inputs_ends(rng):
    at = rng.choice(np.array([0, NT - 1]), (N, 8)); at[:, :2] = 0
    n = lengths(rng, at, rng.integers(2, D + 1, (N, 8))); n[rng.integers(0, N)] = P // NT - 1
    s = starts(n); d = np.choose(rng.integers(0, 6, n.shape), [s * 0 + W, s * 0 + 1, s, s + 1, s + n, n])
    d = inside(rng, n, np.minimum(np.maximum(d, 1), W), 0.5); d[:, 0, 0] = W; d[:, 1, 0] = 1
    return pack(rng, n, fit(n, d))
def setup_inputs_long(rng):
    at = rng.integers(0, NT, (N, 8)); k = rng.integers(P // D, W + 1, (N, 8)); u = rng.integers(0, 3, (N, 8)); k = np.where(u == 0, P // D, np.where(u == 1, W, k))
    for g in range(8):
        q = order(g)[0]; at[q, g] = NT - 1; k[q, g] = rng.integers(P // D, min(W, NT - 1) + 1)
    n = np.zeros((N, 8, NT), np.int64); np.put_along_axis(n, at[:, :, None], P - NT, 2)
    d = rng.integers(1, W + 1, n.shape); np.put_along_axis(d, at[:, :, None], k[:, :, None], 2)
    return pack(rng, n, d)
def setup_inputs_spread(rng):
    d = setup_inputs(rng); d["le"] = wide(rng, N, 128, NT); return d
def check_inputs(d):
    bad = []; a = np.asarray(d["ln"]).astype(np.int64); b = np.asarray(d["ds"]).astype(np.int64)
    if (a < 0).any() or (np.sum(a, 2) + NT != P).any(): bad.append("lengths")
    if (b < 1).any() or (b > W).any(): bad.append("distances")
    if not bad and (steps(a, b) > D).any(): bad.append("steps")
    if not np.isfinite(np.asarray(d["le"]).astype(np.float32)).all(): bad.append("finite")
    return bad
def reference(ln, ds, le):
    y = np.zeros((N, 128, P), BF); t, last = places(ln); t = t.reshape(N, 8, P); last = last.reshape(N, 8, P)
    for g in range(8):
        buf = np.zeros((W + P, 16), BF)
        for r in order(g):
            a = np.ascontiguousarray(le[r, 16 * g:16 * g + 16].T); k = ds[r, g][t[r, g]].tolist(); tk = t[r, g].tolist(); own = last[r, g].tolist()
            for i in range(P):
                buf[W + i] = a[tk[i]] if own[i] else buf[W + i - k[i]]
            y[r, 16 * g:16 * g + 16] = buf[W:].T
            buf[:W] = buf[P:]
    return {"y": y}

@@ -1,0 +1,351 @@
+from concourse.mybir import AluOpType, AxisListType, ActivationFunctionType
+
+P, NT = 2048, 256
+OWN = P
+WIN = OWN + P
+H = P // 2
+ROUNDS = 5
+HI, LO, KC = 9, 10, 11
+SPLIT = 480
+CUT = 320
+BLANK = 3
+COPIED = 1536
+LETTERS = {
+    0: {"b": [(0, 0, NT)]},
+    1: {"b": [(0, 0, NT), (1, 0, NT)]},
+    2: {"b": [(0, 0, NT), (1, 0, NT), (2, 0, NT)]},
+    3: {4: [(3, 0, 128)], 5: [(3, 128, NT)], 6: [(2, 0, 128)], 7: [(2, 128, NT)], 8: [(1, 0, 128)], 9: [(1, 128, NT)],
+        "a": [(0, 0, NT)]},
+}
+
+SCRATCH = {
+    "w0": ("sbuf", [128, WIN], "bfloat16"), "w1": ("sbuf", [128, WIN], "bfloat16"),
+    "tb0": ("sbuf", [128, WIN], "bfloat16"), "tb1": ("sbuf", [128, WIN], "bfloat16"),
+    "tb2": ("sbuf", [128, WIN], "bfloat16"), "tb3": ("sbuf", [128, WIN], "bfloat16"),
+    "tk0": ("sbuf", [128, NT], "bfloat16"), "tk1": ("sbuf", [128, NT], "bfloat16"),
+    "tk2": ("sbuf", [128, NT], "bfloat16"), "tk3": ("sbuf", [128, NT], "bfloat16"),
+    "yo": ("sbuf", [128, P], "bfloat16"),
+    "ll": ("sbuf", [128, 128], "uint16"), "el": ("sbuf", [128, 16], "uint16"), "sl": ("sbuf", [128, 16], "uint16"),
+    "lr0": ("sbuf", [128, 128], "uint16"), "lr1": ("sbuf", [128, 128], "uint16"), "lr2": ("sbuf", [128, 128], "uint16"),
+    "er0": ("sbuf", [128, 16], "uint16"), "er1": ("sbuf", [128, 16], "uint16"), "er2": ("sbuf", [128, 16], "uint16"),
+    "vals": ("sbuf", [128, NT], "bfloat16"), "vend": ("sbuf", [128, NT], "bfloat16"),
+    "x": ("sbuf", [128, 16], "int32"), "dd": ("sbuf", [32, 64], "int32"),
+    "dh": ("sbuf", [32, 64], "bfloat16"), "dl": ("sbuf", [32, 64], "bfloat16"),
+    "jm": ("sbuf", [32, 144], "bfloat16"), "b9": ("sbuf", [32, 144], "bfloat16"),
+    "x1": ("sbuf", [128, 32], "float16"), "xi": ("sbuf", [128, 32], "float16"), "xt": ("sbuf", [128, 32], "float16"),
+    "tot": ("sbuf", [128, 1], "float32"), "u": ("sbuf", [128, 16], "float16"),
+    "ci": ("sbuf", [128, 8], "int32"), "cf": ("sbuf", [128, 8], "float32"), "k11": ("sbuf", [128, 1], "float32"),
+    "p1": ("sbuf", [128, 1], "float32"), "nq": ("sbuf", [128, 1], "float32"), "mk": ("sbuf", [128, 1], "float32"),
+    "ev": ("sbuf", [128, 1], "float32"), "wa": ("sbuf", [128, 1], "float32"), "wr": ("sbuf", [128, 1], "float32"),
+    "e15": ("sbuf", [128, 1], "float32"), "ve": ("sbuf", [128, 1], "float32"),
+    "m1": ("sbuf", [128, 16], "float32"), "m2": ("sbuf", [128, 16], "float32"), "gm": ("sbuf", [128, 128], "bfloat16"),
+    "eye": ("sbuf", [128, 128], "float16"), "eys": ("sbuf", [128, 128], "float16"), "bb": ("sbuf", [128, 128], "float16"),
+    "rm": ("sbuf", [128, 32], "float16"), "ramp": ("sbuf", [128, NT], "bfloat16"), "ee": ("sbuf", [128, 144], "bfloat16"),
+    "pc0": ("psum", [128, 512], "float32"), "pc1": ("psum", [128, 512], "float32"), "pv": ("psum", [128, 512], "float32"),
+    "psy": ("psum", [128, 512], "float32"), "psx": ("psum", [128, 512], "float32"),
+}
+SEMAPHORES = (["qv", "qs", "qp", "qg", "dln", "dds", "dle", "dw0", "dw1", "dw2", "dy0", "dy1", "dy2", "sent"]
+              + ["dz%d" % s for s in range(3)] + ["rle%d" % s for s in range(3)] + ["re%d" % s for s in range(3)]
+              + ["rl%d" % s for s in range(3)] + ["rlb"])
+
+ADD, SUB, MUL, MAX = AluOpType.add, AluOpType.subtract, AluOpType.mult, AluOpType.max
+EQ, NE, GT = AluOpType.is_equal, AluOpType.not_equal, AluOpType.is_gt
+AND, SHR = AluOpType.bitwise_and, AluOpType.logical_shift_right
+AF = ActivationFunctionType
+
+
+def make_tracker(g, T):
+    queues = {"v": g.vector, "s": g.scalar, "p": g.tensor, "g": g, "y": g.sync}
+    known = {e: {} for e in queues}
+    count, clocks, hist = {}, {}, {}
+
+    def record(stream, value, clock, reads, writes):
+        clocks[(stream, value)] = clock
+        for (b, lo, hi) in writes:
+            hist[b] = [h for h in hist.get(b, []) if not (lo <= h[0] and h[1] <= hi)]
+            hist[b].append((lo, hi, True, stream, value))
+        for (b, lo, hi) in reads:
+            hist.setdefault(b, []).append((lo, hi, False, stream, value))
+
+    def wait(e, stream, value):
+        if known[e].get(stream, 0) >= value:
+            return
+        queues[e].wait_ge(T.sem[stream], value)
+        known[e][stream] = value
+        for k, n in clocks.get((stream, value), {}).items():
+            if known[e].get(k, 0) < n:
+                known[e][k] = n
+
+    def ready(e, reads, writes):
+        need = {}
+        for group, w in ((reads, False), (writes, True)):
+            for (b, lo, hi) in group:
+                for h in hist.get(b, []):
+                    if h[0] < hi and lo < h[1] and (h[2] or w):
+                        need[h[3]] = max(need.get(h[3], 0), h[4])
+        for s, n in sorted(need.items(), key=lambda x: -sum(clocks.get(x, {}).values())):
+            wait(e, s, n)
+
+    def op(e, call, reads, writes, stream=None, unit=1):
+        stream = stream or "q" + e
+        ready(e, reads, writes)
+        inst = call(queues[e])
+        inst.then_inc(T.sem[stream], unit)
+        n = count.get(stream, 0) + unit
+        count[stream] = n
+        clock = dict(known[e])
+        clock[stream] = n
+        record(stream, n, clock, reads, writes)
+
+    def arrives(stream, n, b, lo, hi):
+        count[stream] = n
+        record(stream, n, {stream: n}, [], [(b, lo, hi)])
+
+    def finish(e):
+        for s, n in count.items():
+            wait(e, s, n)
+
+    return op, ready, arrives, finish
+
+
+def rank_program(g, core, T, topo):
+    rank = T.rank_of(core)
+    if rank is None:
+        return
+    cores = T.cores
+    end = len(cores) - 1
+    later = list(range(end, rank, -1))
+    op, ready, arrives, finish = make_tracker(g, T)
+    tb = [T["tb%d" % s] for s in range(4)]
+    tbn = ["tb%d" % s for s in range(4)]
+    w = [T.w0, T.w1]
+    wn = ["w0", "w1"]
+
+    def V(call, reads, writes):
+        op("v", call, reads, writes)
+
+    def ts(out, in0, s1, s2, ops, reads, writes):
+        if s2 is None:
+            V(lambda q: q.tensor_scalar(out, in0, s1, None, ops[0]), reads, writes)
+        else:
+            V(lambda q: q.tensor_scalar(out, in0, s1, s2, ops[0], ops[1]), reads, writes)
+
+    def act(out, in_, func, bias, scale, reads, writes):
+        op("s", lambda q: q.activation(out, in_, func, bias=bias, scale=scale), reads, writes)
+
+    def dma(e, stream, out, in_, reads, writes):
+        op(e, lambda q: q.dma_start(out, in_), reads, writes, stream, 16)
+
+    def iota(out, pattern, base, cm, writes, flag=True):
+        if flag:
+            op("g", lambda q: q.iota(out, pattern, base, cm, allow_small_or_imprecise_dtypes=True), [], writes)
+        else:
+            op("g", lambda q: q.iota(out, pattern, base, cm), [], writes)
+
+    def z(lo, hi):
+        return tb[rank][:, OWN + lo:OWN + hi]
+
+    def zt(lo, hi):
+        return (tbn[rank], OWN + lo, OWN + hi)
+
+    def clear(lo, hi):
+        V(lambda q: q.memset(z(lo, hi), 0.0), [], [zt(lo, hi)])
+
+    halves = rank == end
+    for s in range(rank):
+        n = len(topo.engines(cores[s], core))
+        arrives("rle%d" % s, n, "tk%d" % s, 0, NT)
+        arrives("re%d" % s, n, "er%d" % s, 0, 16)
+        if halves and s == 0:
+            arrives("rl0", n, "lr0", 0, 64)
+            arrives("rlb", n, "lr0", 64, 128)
+        else:
+            arrives("rl%d" % s, n, "lr%d" % s, 0, 128)
+
+    dma("y", "dln", T.x[:, :], T.ln[:, :], [], [("x", 0, 16)])
+    dma("s", "dds", T.dd[:, :], T.ds[:, :], [], [("dd", 0, 64)])
+    dma("y", "dle", T["tk%d" % rank][:, :], T.le[:, :], [], [("tk%d" % rank, 0, NT)])
+
+    iota(T.ci[:, 0:1], [[0, 1]], 0, 1, [("ci", 0, 1)], False)
+    iota(T.p1[:, 0:1], [[0, 1]], 1, 1, [("p1", 0, 1)])
+    iota(T.ramp[:, :], [[1, NT]], 0, 0, [("ramp", 0, NT)])
+    iota(T.jm[:, :], [[1, 144]], 0, -4, [("jm", 0, 144)])
+    iota(T.gm[:, :], [[1, 8], [0, 16]], 0, 0, [("gm", 0, 128)])
+    iota(tb[0][:, 0:H], [[0, H]], 0, 0, [("tb0", 0, H)])
+    clear(0, 512)
+    act(z(1024, 1536), z(0, 512), AF.Copy, 0.0, 1.0, [zt(0, 512)], [zt(1024, 1536)])
+    ci0 = [("ci", 0, 1)]
+    ts(T.ci[:, 1:2], T.ci[:, 0:1], 15, None, [AND], ci0, [("ci", 1, 2)])
+    ts(T.ci[:, 2:3], T.ci[:, 0:1], 4, None, [SHR], ci0, [("ci", 2, 3)])
+    ts(T.ci[:, 3:4], T.ci[:, 0:1], 4, 1, [SHR, AND], ci0, [("ci", 3, 4)])
+    clear(512, 1024)
+    V(lambda q: q.tensor_copy(T.cf[:, 1:4], T.ci[:, 1:4]), [("ci", 1, 4)], [("cf", 1, 4)])
+    qcol, gcol, odd = T.cf[:, 1:2], T.cf[:, 2:3], T.cf[:, 3:4]
+    cf = ("cf", 1, 4)
+    rp = ("ramp", 0, NT)
+    ts(T.nq[:, :], qcol, 15.0, None, [NE], [cf], [("nq", 0, 1)])
+    ts(T.m1[:, :], T.ramp[:, 0:16], qcol, None, [EQ], [cf, rp], [("m1", 0, 16)])
+    ts(T.m2[:, :], T.ramp[:, 0:16], qcol, 256.0, [GT, MUL], [cf, rp], [("m2", 0, 16)])
+    act(T.ev[:, :], odd, AF.Identity, 1.0, -1.0, [cf], [("ev", 0, 1)])
+    act(T.wa[:, :], qcol, AF.Abs, -9.5, 1.0, [cf], [("wa", 0, 1)])
+    act(T.e15[:, :], gcol, AF.Identity, 15.0, 16.0, [cf], [("e15", 0, 1)])
+    act(T.wr[:, :], T.wa[:, :], AF.Sign, -1.0, 1.0, [("wa", 0, 1)], [("wr", 0, 1)])
+
+    def ramp_block(b):
+        act(T.w0[:, 256 * b:256 * b + 256], T.ramp[:, :], AF.Identity, T.m2[:, b:b + 1], T.m1[:, b:b + 1],
+            [rp, ("m1", 0, 16), ("m2", 0, 16)], [("w0", 256 * b, 256 * b + 256)])
+    ramp_block(0)
+    act(T.mk[:, :], T.wr[:, :], AF.Identity, 0.5, -0.5, [("wr", 0, 1)], [("mk", 0, 1)])
+    act(T.ve[:, :], T.wr[:, :], AF.Identity, -2048.0, 2048.0, [("wr", 0, 1)], [("ve", 0, 1)])
+    act(T.vend[:, :], T.ramp[:, :], AF.Identity, T.ve[:, 0:1], 0.0, [rp, ("ve", 0, 1)], [("vend", 0, NT)])
+    ramp_block(1)
+    ts(T.rm[:, :], T.ramp[:, 0:32], 16.0, None, [NE], [rp], [("rm", 0, 32)])
+    ts(T.eye[:, :], T.ramp[:, 1:129], T.p1[:, 0:1], None, [EQ], [rp, ("p1", 0, 1)], [("eye", 0, 128)])
+    ts(T.eys[:, :], T.ramp[:, 0:128], T.p1[:, 0:1], T.nq[:, 0:1], [EQ, MUL], [rp, ("p1", 0, 1), ("nq", 0, 1)],
+       [("eys", 0, 128)])
+    ts(T.b9[:, :], T.jm[:, :], float(LO), None, [EQ], [("jm", 0, 144)], [("b9", 0, 144)])
+
+    ts(T.x1[:, 0:16], T.x[:, :], 1.0, T.ev[:, 0:1], [ADD, MUL], [("x", 0, 16), ("ev", 0, 1)], [("x1", 0, 16)])
+    ts(T.x1[:, 16:32], T.x[:, :], 1.0, odd, [ADD, MUL], [("x", 0, 16), cf], [("x1", 16, 32)])
+    ts(T.dh[:, :], T.dd[:, :], -4.0, 0.0, [ADD, MAX], [("dd", 0, 64)], [("dh", 0, 64)])
+    V(lambda q: q.tensor_tensor_scan(T.xi[:, :], T.rm[:, :], T.x1[:, :], 0.0, MUL, ADD),
+      [("rm", 0, 32), ("x1", 0, 32)], [("xi", 0, 32)])
+    V(lambda q: q.tensor_tensor(T.dl[:, :], T.dd[:, :], T.dh[:, :], SUB), [("dd", 0, 64), ("dh", 0, 64)], [("dl", 0, 64)])
+    V(lambda q: q.tensor_reduce(T.tot[:, :], T.x1[:, :], AxisListType.X, ADD), [("x1", 0, 32)], [("tot", 0, 1)])
+    ts(T.bb[:, :], T.gm[:, :], gcol, None, [EQ], [("gm", 0, 128), cf], [("bb", 0, 128)])
+    V(lambda q: q.transpose(T.xt[:, :], T.xi[:, :]), [("xi", 0, 32)], [("xt", 0, 32)])
+    ts(T.u[:, :], T.m2[:, :], T.tot[:, 0:1], 1.0 / 256, [MUL, MUL], [("m2", 0, 16), ("tot", 0, 1)], [("u", 0, 16)])
+
+    def dist(q):
+        for a in range(4):
+            q.matmul(T.pv[:, 64 * a:64 * a + 64], T.b9[:, 4 * a + 1:4 * a + 129], T.dh[:, :], True, False)
+            i = q.matmul(T.pv[:, 64 * a:64 * a + 64], T.b9[:, 4 * a:4 * a + 128], T.dl[:, :], False, True)
+        return i
+    op("p", dist, [("b9", 0, 144), ("dh", 0, 64), ("dl", 0, 64)], [("pv", 0, NT)])
+
+    def sums(ps, name, ey, eyn):
+        def call(q):
+            q.matmul(ps[:, 0:16], ey[:, :], T.xt[:, 0:16], True, False)
+            q.matmul(ps[:, 0:16], ey[:, :], T.xt[:, 16:32], False, False)
+            return q.matmul(ps[:, 0:16], T.bb[:, :], T.u[:, :], False, True)
+        op("p", call, [(eyn, 0, 128), ("bb", 0, 128), ("xt", 0, 32), ("u", 0, 16)], [(name, 0, 16)])
+    sums(T.psy, "psy", T.eys, "eys")
+    sums(T.psx, "psx", T.eye, "eye")
+    act(T.vals[:, :], T.pv[:, 0:NT], AF.Identity, 0.0, T.mk[:, 0:1], [("pv", 0, NT), ("mk", 0, 1)], [("vals", 0, NT)])
+    for b in range(2, 8):
+        ramp_block(b)
+    act(T.w1[:, COPIED:OWN], T.w0[:, COPIED:OWN], AF.Copy, 0.0, 1.0, [("w0", COPIED, OWN)], [("w1", COPIED, OWN)])
+    for k in range(COPIED // 512):
+        lo, hi = 512 * k, 512 * k + 512
+        dma("y", "dw%d" % k, T.w1[:, lo:hi], T.w0[:, lo:hi], [("w0", lo, hi)], [("w1", lo, hi)])
+    clear(1536, 2048)
+    V(lambda q: q.tensor_copy(T.sl[:, :], T.psy[:, 0:16]), [("psy", 0, 16)], [("sl", 0, 16)])
+    ts(T.el[:, :], T.psx[:, 0:16], -1.0, None, [ADD], [("psx", 0, 16)], [("el", 0, 16)])
+    ts(T.k11[:, :], qcol, float(KC), float(OWN), [EQ, MUL], [cf], [("k11", 0, 1)])
+
+    V(lambda q: q.tensor_copy(z(0, P).indirect(T.sl[:, 0:16]), T.vals[:, :]), [("sl", 0, 16), ("vals", 0, NT)], [zt(0, P)])
+    ts(T.ee[:, :], T.ramp[:, 0:144], T.e15[:, 0:1], T.wr[:, 0:1], [EQ, MUL], [rp, ("e15", 0, 1), ("wr", 0, 1)],
+       [("ee", 0, 144)])
+    V(lambda q: q.tensor_copy(z(0, P).indirect(T.el[:, 0:16]), T.vend[:, :]), [("el", 0, 16), ("vend", 0, NT)], [zt(0, P)])
+
+    def pointers(h):
+        lo, hi = H * h, H * h + H
+        if h:
+            ini, r = T.w0[:, OWN + lo - 1:OWN + lo], ("w0", OWN + lo - 1, OWN + lo)
+        else:
+            ini, r = T.k11[:, 0:1], ("k11", 0, 1)
+        V(lambda q: q.tensor_tensor_scan(T.w0[:, OWN + lo:OWN + hi], z(lo, hi), T.w0[:, lo:hi], ini, ADD, MAX),
+          [zt(lo, hi), ("w0", lo, hi), r], [("w0", OWN + lo, OWN + hi)])
+
+    sent = [0]
+
+    def send(to, out, in_, sem, reads):
+        ready("g", reads, [])
+        for r in to:
+            rid, pid = topo.addr(cores[r])[:2]
+            g.remote_dma(out_ap=out, in_ap=in_, remote_sem=T.sem[sem], local_sem=T.sem.sent, pid=pid, routing_id=rid,
+                         dma_engine_mask=topo.mask(core, cores[r]))
+            sent[0] += len(topo.engines(core, cores[r]))
+    if later:
+        ready("g", [("w0", 0, COPIED)], [])
+    for r in later:
+        send([r], T["tk%d" % rank][:, :], T["tk%d" % rank][:, :], "rle%d" % rank, [("tk%d" % rank, 0, NT)])
+        send([r], T["er%d" % rank][:, :], T.el[:, :], "re%d" % rank, [("el", 0, 16)])
+
+    def blank():
+        for k, lo in enumerate([H] + ([OWN, OWN + H] if rank else [])):
+            dma("y", "dz%d" % k, tb[0][:, lo:lo + H], tb[0][:, 0:H], [("tb0", 0, H)], [("tb0", lo, lo + H)])
+    for s in range(rank - 1, 0, -1):
+        iota(tb[s][:, OWN:WIN], [[0, P]], 0, 0, [(tbn[s], OWN, WIN)])
+    if not later:
+        blank()
+
+    pc, pcn = [T.pc0, T.pc1], ["pc0", "pc1"]
+
+    def letters(k):
+        for s, lo, hi in LETTERS[rank].get(k, []):
+            name, src = "er%d" % s if s < rank else "el", T["tk%d" % s]
+            V(lambda q: q.tensor_copy(tb[s][:, OWN:WIN].indirect(T[name][:, lo // 16:hi // 16]), src[:, lo:hi]),
+              [(name, 0, 16), ("tk%d" % s, lo, hi)], [(tbn[s], OWN, WIN)])
+
+    def spread(k, h):
+        lo = OWN + H * h
+
+        def call(q):
+            for j in range(16):
+                i = q.matmul(pc[h][:, 0:64], T.ee[:, 15 - j:143 - j], w[k][:, lo + j:lo + H:16], j == 0, j == 15)
+            return i
+        op("p", call, [(wn[k], lo, lo + H), ("ee", 0, 144)], [(pcn[h], 0, 64)])
+
+    def listed(h):
+        V(lambda q: q.tensor_copy(T.ll[:, 64 * h:64 * h + 64], pc[h][:, 0:64]), [(pcn[h], 0, 64)], [("ll", 64 * h, 64 * h + 64)])
+
+    def gather(e, out, outn, off, win, winn, top, lst, lstn, lo, hi):
+        o, src = out[:, off + lo:off + hi], win[:, 0:top].indirect(lst[:, lo // 16:hi // 16])
+        rd, wr = [(winn, 0, top), (lstn, lo // 16, hi // 16)], [(outn, off + lo, off + hi)]
+        if e == "v":
+            V(lambda q: q.tensor_copy(o, src), rd, wr)
+        else:
+            op("s", lambda q: q.activation(o, src, AF.Copy), rd, wr)
+    pointers(0)
+    spread(0, 0)
+    pointers(1)
+    spread(0, 1)
+    for r in range(ROUNDS):
+        a, b = r % 2, (r + 1) % 2
+        for h in range(2):
+            lo, k = H * h, 2 * r + h
+            top = OWN + lo + H
+            mid = lo + (CUT if k in LETTERS[rank] else SPLIT)
+            listed(h)
+            gather("s", w[b], wn[b], OWN, w[a], wn[a], top, T.ll, "ll", mid, lo + H)
+            gather("v", w[b], wn[b], OWN, w[a], wn[a], top, T.ll, "ll", lo, mid)
+            spread(b, h)
+            letters(k)
+            if k == BLANK and later:
+                ready("y", [(wn[b], OWN + lo, OWN + mid)], [])
+                blank()
+    listed(0)
+    if rank == 0:
+        send([end], T.lr0[:, 0:64], T.ll[:, 0:64], "rl0", [("ll", 0, 64)])
+    letters("a")
+    listed(1)
+    if rank == 0:
+        send([end], T.lr0[:, 64:128], T.ll[:, 64:128], "rlb", [("ll", 64, 128)])
+        send(later[1:], T.lr0[:, :], T.ll[:, :], "rl0", [("ll", 0, 128)])
+    elif later:
+        send(later, T["lr%d" % rank][:, :], T.ll[:, :], "rl%d" % rank, [("ll", 0, 128)])
+
+    letters("b")
+    for s in range(rank):
+        n = H if halves and s == 0 else P
+        for lo in range(0, P, n):
+            for e, d in (("v", 0), ("s", n // 2)):
+                gather(e, tb[s + 1], tbn[s + 1], 0, tb[s], tbn[s], WIN, T["lr%d" % s], "lr%d" % s, lo + d, lo + d + n // 2)
+    for k, (lo, n) in enumerate(((0, 1024), (1024, 512), (1536, 512))):
+        for e, d in (("v", 0), ("s", n // 2)):
+            gather(e, T.yo, "yo", 0, tb[rank], tbn[rank], WIN, T.ll, "ll", lo + d, lo + d + n // 2)
+        dma("y", "dy%d" % k, T.y[:, lo:lo + n], T.yo[:, lo:lo + n], [("yo", lo, lo + n)], [("y", lo, lo + n)])
+    if later:
+        g.wait_ge(T.sem.sent, sent[0])
+    finish("y")

@@ -1,22 +1,27 @@
-from concourse.mybir import AluOpType, AxisListType, ActivationFunctionType
+from concourse.mybir import AluOpType, ActivationFunctionType
 
 P, NT = 2048, 256
 OWN = P
 WIN = OWN + P
-H = P // 2
 ROUNDS = 5
-HI, LO, KC = 9, 10, 11
+BIG = 4096.0
+FIRST = OWN - 16
+BLOCKS = ((0, 1024), (1024, 2048))
 SPLIT = 480
-CUT = 320
-BLANK = 3
-COPIED = 1536
-LETTERS = {
-    0: {"b": [(0, 0, NT)]},
-    1: {"b": [(0, 0, NT), (1, 0, NT)]},
-    2: {"b": [(0, 0, NT), (1, 0, NT), (2, 0, NT)]},
-    3: {4: [(3, 0, 128)], 5: [(3, 128, NT)], 6: [(2, 0, 128)], 7: [(2, 128, NT)], 8: [(1, 0, 128)], 9: [(1, 128, NT)],
-        "a": [(0, 0, NT)]},
-}
+STORES = ((0, 512, "y"), (512, 1024, "y"), (1536, 512, "s"))
+LETTERS = {0: {"l1": [(0, 0, 256)]},
+           1: {"l1": [(0, 0, 256), (1, 0, 256)]},
+           2: {"l0": [(2, 0, 256)], "l1": [(0, 0, 256), (1, 0, 256)]},
+           3: {0: [(3, 0, 96)], 1: [(3, 96, 192)], 2: [(3, 192, 256)], 5: [(0, 0, 96)], 6: [(0, 96, 192)],
+               7: [(0, 192, 256)], 8: [(1, 0, 96)], 9: [(1, 96, 192)], "l0": [(1, 192, 256), (2, 0, 160)],
+               "l1": [(2, 160, 256)]}}
+CUT = 384
+BYBLOCK = (3,)
+ORDER = ("ci ones and ramp twos zc oh zs0 g2 dp0 wd nb sc gcol m2 dh kc e8 bi x1 dl zs1 sums zv3 wr dist r0 r1 ends zv2 "
+         "vals s0b copy s0c s0d s1c s1d ee el")
+ORDER0 = ("ci ones and ramp twos zc oh zs0 g2 dp0 wd nb sc gcol m2 dh kc e8 bi x1 dl zs1 sums zv3 wr dist r0 r1 ends zv2 "
+          "vals s0b s0c s0d ee el")
+SPLIT0 = 512
 
 SCRATCH = {
     "w0": ("sbuf", [128, WIN], "bfloat16"), "w1": ("sbuf", [128, WIN], "bfloat16"),
@@ -25,32 +30,27 @@ SCRATCH = {
     "tk0": ("sbuf", [128, NT], "bfloat16"), "tk1": ("sbuf", [128, NT], "bfloat16"),
     "tk2": ("sbuf", [128, NT], "bfloat16"), "tk3": ("sbuf", [128, NT], "bfloat16"),
     "yo": ("sbuf", [128, P], "bfloat16"),
-    "ll": ("sbuf", [128, 128], "uint16"), "el": ("sbuf", [128, 16], "uint16"), "sl": ("sbuf", [128, 16], "uint16"),
+    "ll": ("sbuf", [128, 128], "uint16"), "el": ("sbuf", [128, 16], "uint16"),
     "lr0": ("sbuf", [128, 128], "uint16"), "lr1": ("sbuf", [128, 128], "uint16"), "lr2": ("sbuf", [128, 128], "uint16"),
     "er0": ("sbuf", [128, 16], "uint16"), "er1": ("sbuf", [128, 16], "uint16"), "er2": ("sbuf", [128, 16], "uint16"),
-    "vals": ("sbuf", [128, NT], "bfloat16"), "vend": ("sbuf", [128, NT], "bfloat16"),
-    "x": ("sbuf", [128, 16], "int32"), "dd": ("sbuf", [32, 64], "int32"),
-    "dh": ("sbuf", [32, 64], "bfloat16"), "dl": ("sbuf", [32, 64], "bfloat16"),
-    "jm": ("sbuf", [32, 144], "bfloat16"), "b9": ("sbuf", [32, 144], "bfloat16"),
-    "x1": ("sbuf", [128, 32], "float16"), "xi": ("sbuf", [128, 32], "float16"), "xt": ("sbuf", [128, 32], "float16"),
-    "tot": ("sbuf", [128, 1], "float32"), "u": ("sbuf", [128, 16], "float16"),
-    "ci": ("sbuf", [128, 8], "int32"), "cf": ("sbuf", [128, 8], "float32"), "k11": ("sbuf", [128, 1], "float32"),
-    "p1": ("sbuf", [128, 1], "float32"), "nq": ("sbuf", [128, 1], "float32"), "mk": ("sbuf", [128, 1], "float32"),
-    "ev": ("sbuf", [128, 1], "float32"), "wa": ("sbuf", [128, 1], "float32"), "wr": ("sbuf", [128, 1], "float32"),
-    "e15": ("sbuf", [128, 1], "float32"), "ve": ("sbuf", [128, 1], "float32"),
-    "m1": ("sbuf", [128, 16], "float32"), "m2": ("sbuf", [128, 16], "float32"), "gm": ("sbuf", [128, 128], "bfloat16"),
-    "eye": ("sbuf", [128, 128], "float16"), "eys": ("sbuf", [128, 128], "float16"), "bb": ("sbuf", [128, 128], "float16"),
-    "rm": ("sbuf", [128, 32], "float16"), "ramp": ("sbuf", [128, NT], "bfloat16"), "ee": ("sbuf", [128, 144], "bfloat16"),
-    "pc0": ("psum", [128, 512], "float32"), "pc1": ("psum", [128, 512], "float32"), "pv": ("psum", [128, 512], "float32"),
-    "psy": ("psum", [128, 512], "float32"), "psx": ("psum", [128, 512], "float32"),
+    "vals": ("sbuf", [128, NT], "bfloat16"), "ini": ("sbuf", [128, 2], "bfloat16"),
+    "x": ("sbuf", [8, NT], "int32"), "x1": ("sbuf", [8, NT], "float16"), "xi": ("sbuf", [8, NT], "float16"),
+    "dd": ("sbuf", [16, 128], "int32"), "dp": ("sbuf", [48, 130], "bfloat16"), "wd": ("sbuf", [48, 144], "bfloat16"),
+    "e8": ("sbuf", [8, 144], "float16"), "ee": ("sbuf", [128, 144], "bfloat16"),
+    "ci": ("sbuf", [128, 16], "int32"), "g2": ("sbuf", [128, 2], "bfloat16"), "cc": ("sbuf", [128, 16], "bfloat16"),
+    "oh": ("sbuf", [128, 8], "bfloat16"), "m2": ("sbuf", [128, 8], "bfloat16"), "sc": ("sbuf", [128, 2], "float32"),
+    "ramp": ("sbuf", [128, NT], "bfloat16"), "ones": ("sbuf", [128, 512], "bfloat16"),
+    "twos": ("sbuf", [48, 144], "bfloat16"),
+    "pc0": ("psum", [128, 512], "float32"), "pc1": ("psum", [128, 512], "float32"), "pc2": ("psum", [128, 512], "float32"),
+    "pv": ("psum", [128, 512], "float32"), "psx": ("psum", [128, 512], "float32"),
 }
-SEMAPHORES = (["qv", "qs", "qp", "qg", "dln", "dds", "dle", "dw0", "dw1", "dw2", "dy0", "dy1", "dy2", "sent"]
-              + ["dz%d" % s for s in range(3)] + ["rle%d" % s for s in range(3)] + ["re%d" % s for s in range(3)]
-              + ["rl%d" % s for s in range(3)] + ["rlb"])
+SEMAPHORES = (["qv", "qs", "qp", "qg", "dln", "dds", "dle", "dz", "dw", "sent"]
+              + ["dy%d" % k for k in range(len(STORES))]
+              + ["rle%d" % s for s in range(3)] + ["re%d" % s for s in range(3)]
+              + ["rl%d" % s for s in range(3)] + ["rb%d" % b for b in range(len(BLOCKS))])
 
 ADD, SUB, MUL, MAX = AluOpType.add, AluOpType.subtract, AluOpType.mult, AluOpType.max
-EQ, NE, GT = AluOpType.is_equal, AluOpType.not_equal, AluOpType.is_gt
-AND, SHR = AluOpType.bitwise_and, AluOpType.logical_shift_right
+EQ, LT, AND = AluOpType.is_equal, AluOpType.is_lt, AluOpType.bitwise_and
 AF = ActivationFunctionType
 
 
@@ -116,10 +116,10 @@ def rank_program(g, core, T, topo):
     end = len(cores) - 1
     later = list(range(end, rank, -1))
     op, ready, arrives, finish = make_tracker(g, T)
-    tb = [T["tb%d" % s] for s in range(4)]
-    tbn = ["tb%d" % s for s in range(4)]
     w = [T.w0, T.w1]
     wn = ["w0", "w1"]
+    tbn = ["tb%d" % s if s == rank or not later else wn[s] for s in range(rank + 1)]
+    tb = [T[n] for n in tbn]
 
     def V(call, reads, writes):
         op("v", call, reads, writes)
@@ -130,8 +130,8 @@ def rank_program(g, core, T, topo):
         else:
             V(lambda q: q.tensor_scalar(out, in0, s1, s2, ops[0], ops[1]), reads, writes)
 
-    def act(out, in_, func, bias, scale, reads, writes):
-        op("s", lambda q: q.activation(out, in_, func, bias=bias, scale=scale), reads, writes)
+    def act(out, in_, bias, scale, reads, writes):
+        op("s", lambda q: q.activation(out, in_, AF.Identity, bias=bias, scale=scale), reads, writes)
 
     def dma(e, stream, out, in_, reads, writes):
         op(e, lambda q: q.dma_start(out, in_), reads, writes, stream, 16)
@@ -142,120 +142,131 @@ def rank_program(g, core, T, topo):
         else:
             op("g", lambda q: q.iota(out, pattern, base, cm), [], writes)
 
+    def select(out, in_, pattern, base, cm, reads, writes):
+        op("g", lambda q: q.affine_select(out, in_, pattern, EQ, 0.0, base, cm), reads, writes)
+
     def z(lo, hi):
         return tb[rank][:, OWN + lo:OWN + hi]
 
     def zt(lo, hi):
         return (tbn[rank], OWN + lo, OWN + hi)
 
-    def clear(lo, hi):
-        V(lambda q: q.memset(z(lo, hi), 0.0), [], [zt(lo, hi)])
-
-    halves = rank == end
     for s in range(rank):
         n = len(topo.engines(cores[s], core))
         arrives("rle%d" % s, n, "tk%d" % s, 0, NT)
         arrives("re%d" % s, n, "er%d" % s, 0, 16)
-        if halves and s == 0:
-            arrives("rl0", n, "lr0", 0, 64)
-            arrives("rlb", n, "lr0", 64, 128)
+        if rank in BYBLOCK and s == 0:
+            for b, (lo, hi) in enumerate(BLOCKS):
+                arrives("rb%d" % b, n, "lr0", lo // 16, hi // 16)
         else:
             arrives("rl%d" % s, n, "lr%d" % s, 0, 128)
 
-    dma("y", "dln", T.x[:, :], T.ln[:, :], [], [("x", 0, 16)])
-    dma("s", "dds", T.dd[:, :], T.ds[:, :], [], [("dd", 0, 64)])
+    dma("s", "dds", T.dd[:, :], T.ds[:, :], [], [("dd", 0, 128)])
+    dma("y", "dln", T.x[:, :], T.ln[:, :], [], [("x", 0, NT)])
     dma("y", "dle", T["tk%d" % rank][:, :], T.le[:, :], [], [("tk%d" % rank, 0, NT)])
 
-    iota(T.ci[:, 0:1], [[0, 1]], 0, 1, [("ci", 0, 1)], False)
-    iota(T.p1[:, 0:1], [[0, 1]], 1, 1, [("p1", 0, 1)])
-    iota(T.ramp[:, :], [[1, NT]], 0, 0, [("ramp", 0, NT)])
-    iota(T.jm[:, :], [[1, 144]], 0, -4, [("jm", 0, 144)])
-    iota(T.gm[:, :], [[1, 8], [0, 16]], 0, 0, [("gm", 0, 128)])
-    iota(tb[0][:, 0:H], [[0, H]], 0, 0, [("tb0", 0, H)])
-    clear(0, 512)
-    act(z(1024, 1536), z(0, 512), AF.Copy, 0.0, 1.0, [zt(0, 512)], [zt(1024, 1536)])
-    ci0 = [("ci", 0, 1)]
-    ts(T.ci[:, 1:2], T.ci[:, 0:1], 15, None, [AND], ci0, [("ci", 1, 2)])
-    ts(T.ci[:, 2:3], T.ci[:, 0:1], 4, None, [SHR], ci0, [("ci", 2, 3)])
-    ts(T.ci[:, 3:4], T.ci[:, 0:1], 4, 1, [SHR, AND], ci0, [("ci", 3, 4)])
-    clear(512, 1024)
-    V(lambda q: q.tensor_copy(T.cf[:, 1:4], T.ci[:, 1:4]), [("ci", 1, 4)], [("cf", 1, 4)])
-    qcol, gcol, odd = T.cf[:, 1:2], T.cf[:, 2:3], T.cf[:, 3:4]
-    cf = ("cf", 1, 4)
-    rp = ("ramp", 0, NT)
-    ts(T.nq[:, :], qcol, 15.0, None, [NE], [cf], [("nq", 0, 1)])
-    ts(T.m1[:, :], T.ramp[:, 0:16], qcol, None, [EQ], [cf, rp], [("m1", 0, 16)])
-    ts(T.m2[:, :], T.ramp[:, 0:16], qcol, 256.0, [GT, MUL], [cf, rp], [("m2", 0, 16)])
-    act(T.ev[:, :], odd, AF.Identity, 1.0, -1.0, [cf], [("ev", 0, 1)])
-    act(T.wa[:, :], qcol, AF.Abs, -9.5, 1.0, [cf], [("wa", 0, 1)])
-    act(T.e15[:, :], gcol, AF.Identity, 15.0, 16.0, [cf], [("e15", 0, 1)])
-    act(T.wr[:, :], T.wa[:, :], AF.Sign, -1.0, 1.0, [("wa", 0, 1)], [("wr", 0, 1)])
+    def column(k, n=1):
+        return T.cc[:, k:k + n], ("cc", k, k + n)
+    zc, zcn = column(0)
+    wr, wrn = column(1)
+    sc, scn = T.sc[:, :], ("sc", 0, 2)
+    nb, nbn = column(4)
+    kc, kcn = column(5)
+    bi, bin_ = column(6, 2)
+    gcol, gcn = column(8)
+    one, rp, dp, cb, ohn = ("ones", 0, 512), ("ramp", 0, NT), ("dp", 0, 130), ("ci", 8, 16), ("oh", 0, 8)
+    two = ("twos", 0, 144)
+
+    def fill(e, k):
+        lo, hi = 512 * k, 512 * k + 512
+        if e == "s":
+            act(z(lo, hi), T.ones[:, :], zc, 0.0, [one, zcn], [zt(lo, hi)])
+        elif e == "v":
+            ts(z(lo, hi), T.ones[:, :], zc, None, [MUL], [one, zcn], [zt(lo, hi)])
+        else:
+            select(z(lo, hi), z(0, 512), [[0, 512]], 0, 0, [zt(0, 512)], [zt(lo, hi)])
+
+    fixn = wn if rank else ["yo"]
+    fix = [T[n] for n in fixn]
+    base = [FIRST] + [0] * end
 
     def ramp_block(b):
-        act(T.w0[:, 256 * b:256 * b + 256], T.ramp[:, :], AF.Identity, T.m2[:, b:b + 1], T.m1[:, b:b + 1],
-            [rp, ("m1", 0, 16), ("m2", 0, 16)], [("w0", 256 * b, 256 * b + 256)])
-    ramp_block(0)
-    act(T.mk[:, :], T.wr[:, :], AF.Identity, 0.5, -0.5, [("wr", 0, 1)], [("mk", 0, 1)])
-    act(T.ve[:, :], T.wr[:, :], AF.Identity, -2048.0, 2048.0, [("wr", 0, 1)], [("ve", 0, 1)])
-    act(T.vend[:, :], T.ramp[:, :], AF.Identity, T.ve[:, 0:1], 0.0, [rp, ("ve", 0, 1)], [("vend", 0, NT)])
-    ramp_block(1)
-    ts(T.rm[:, :], T.ramp[:, 0:32], 16.0, None, [NE], [rp], [("rm", 0, 32)])
-    ts(T.eye[:, :], T.ramp[:, 1:129], T.p1[:, 0:1], None, [EQ], [rp, ("p1", 0, 1)], [("eye", 0, 128)])
-    ts(T.eys[:, :], T.ramp[:, 0:128], T.p1[:, 0:1], T.nq[:, 0:1], [EQ, MUL], [rp, ("p1", 0, 1), ("nq", 0, 1)],
-       [("eys", 0, 128)])
-    ts(T.b9[:, :], T.jm[:, :], float(LO), None, [EQ], [("jm", 0, 144)], [("b9", 0, 144)])
+        ts(fix[0][:, 256 * b:256 * b + 256], T.ramp[:, :], T.oh[:, 0:1], T.m2[:, b:b + 1], [MUL, ADD],
+           [rp, ohn, ("m2", 0, 8)], [(fixn[0], 256 * b, 256 * b + 256)])
 
-    ts(T.x1[:, 0:16], T.x[:, :], 1.0, T.ev[:, 0:1], [ADD, MUL], [("x", 0, 16), ("ev", 0, 1)], [("x1", 0, 16)])
-    ts(T.x1[:, 16:32], T.x[:, :], 1.0, odd, [ADD, MUL], [("x", 0, 16), cf], [("x1", 16, 32)])
-    ts(T.dh[:, :], T.dd[:, :], -4.0, 0.0, [ADD, MAX], [("dd", 0, 64)], [("dh", 0, 64)])
-    V(lambda q: q.tensor_tensor_scan(T.xi[:, :], T.rm[:, :], T.x1[:, :], 0.0, MUL, ADD),
-      [("rm", 0, 32), ("x1", 0, 32)], [("xi", 0, 32)])
-    V(lambda q: q.tensor_tensor(T.dl[:, :], T.dd[:, :], T.dh[:, :], SUB), [("dd", 0, 64), ("dh", 0, 64)], [("dl", 0, 64)])
-    V(lambda q: q.tensor_reduce(T.tot[:, :], T.x1[:, :], AxisListType.X, ADD), [("x1", 0, 32)], [("tot", 0, 1)])
-    ts(T.bb[:, :], T.gm[:, :], gcol, None, [EQ], [("gm", 0, 128), cf], [("bb", 0, 128)])
-    V(lambda q: q.transpose(T.xt[:, :], T.xi[:, :]), [("xi", 0, 32)], [("xt", 0, 32)])
-    ts(T.u[:, :], T.m2[:, :], T.tot[:, 0:1], 1.0 / 256, [MUL, MUL], [("m2", 0, 16), ("tot", 0, 1)], [("u", 0, 16)])
+    def shifted(e, k, lo):
+        rd, wt, c = [(fixn[0], 0, 512), ("m2", 0, 8)], [(fixn[k], lo, lo + 512)], T.m2[:, lo // 256:lo // 256 + 1]
+        if e == "s":
+            act(fix[k][:, lo:lo + 512], fix[0][:, 0:512], c, 1.0, rd, wt)
+        else:
+            ts(fix[k][:, lo:lo + 512], fix[0][:, 0:512], c, None, [ADD], rd, wt)
 
     def dist(q):
-        for a in range(4):
-            q.matmul(T.pv[:, 64 * a:64 * a + 64], T.b9[:, 4 * a + 1:4 * a + 129], T.dh[:, :], True, False)
-            i = q.matmul(T.pv[:, 64 * a:64 * a + 64], T.b9[:, 4 * a:4 * a + 128], T.dl[:, :], False, True)
+        q.matmul(T.pv[:, 0:128], T.wd[:, 8:136], T.dp[:, 0:128], True, True)
+        return q.matmul(T.pv[:, 128:NT + 2], T.wd[:, 16:144], T.dp[:, :], True, True)
+
+    def ends(q):
+        for j in range(16):
+            i = q.matmul(T.psx[:, 0:16], T.e8[:, 15 - j:143 - j], T.xi[:, j:NT:16], j == 0, j == 15)
         return i
-    op("p", dist, [("b9", 0, 144), ("dh", 0, 64), ("dl", 0, 64)], [("pv", 0, NT)])
 
-    def sums(ps, name, ey, eyn):
-        def call(q):
-            q.matmul(ps[:, 0:16], ey[:, :], T.xt[:, 0:16], True, False)
-            q.matmul(ps[:, 0:16], ey[:, :], T.xt[:, 16:32], False, False)
-            return q.matmul(ps[:, 0:16], T.bb[:, :], T.u[:, :], False, True)
-        op("p", call, [(eyn, 0, 128), ("bb", 0, 128), ("xt", 0, 32), ("u", 0, 16)], [(name, 0, 16)])
-    sums(T.psy, "psy", T.eys, "eys")
-    sums(T.psx, "psx", T.eye, "eye")
-    act(T.vals[:, :], T.pv[:, 0:NT], AF.Identity, 0.0, T.mk[:, 0:1], [("pv", 0, NT), ("mk", 0, 1)], [("vals", 0, NT)])
-    for b in range(2, 8):
-        ramp_block(b)
-    act(T.w1[:, COPIED:OWN], T.w0[:, COPIED:OWN], AF.Copy, 0.0, 1.0, [("w0", COPIED, OWN)], [("w1", COPIED, OWN)])
-    for k in range(COPIED // 512):
-        lo, hi = 512 * k, 512 * k + 512
-        dma("y", "dw%d" % k, T.w1[:, lo:hi], T.w0[:, lo:hi], [("w0", lo, hi)], [("w1", lo, hi)])
-    clear(1536, 2048)
-    V(lambda q: q.tensor_copy(T.sl[:, :], T.psy[:, 0:16]), [("psy", 0, 16)], [("sl", 0, 16)])
-    ts(T.el[:, :], T.psx[:, 0:16], -1.0, None, [ADD], [("psx", 0, 16)], [("el", 0, 16)])
-    ts(T.k11[:, :], qcol, float(KC), float(OWN), [EQ, MUL], [cf], [("k11", 0, 1)])
+    def values():
+        for par in range(2):
+            c = 1 - par
+            act(T.vals[:, par:NT:2], T.pv[:, par + 1:NT + 1:2], T.cc[:, 6 + c:7 + c], T.sc[:, c:c + 1],
+                [("pv", 0, NT + 2), scn, bin_], [("vals", par, par + 1)])
+        act(T.ini[:, 0:1], T.pv[:, 0:1], kc, T.sc[:, 0:1], [("pv", 0, NT + 2), scn, kcn], [("ini", 0, 1)])
+    steps = {
+        "ones": lambda: V(lambda q: q.memset(T.ones[:, :], 1.0), [], [one]),
+        "twos": lambda: iota(T.twos[:, :], [[0, 144]], 2, 0, [two]),
+        "dp0": lambda: V(lambda q: q.memset(T.dp[:, :], 0.0), [], [dp]),
+        "ramp": lambda: V(lambda q: q.tensor_tensor_scan(T.ramp[:, :], T.ones[:, 0:NT], T.ones[:, 0:NT], -1.0, ADD, MUL),
+                          [one], [rp]),
+        "ci": lambda: iota(T.ci[:, 0:8], [[-2, 8]], 16, 1, [("ci", 0, 8)], False),
+        "wd": lambda: select(T.wd[:, :], T.twos[:, :], [[1, 18], [0, 4], [32, 2]], -2, -1, [two], [("wd", 0, 144)]),
+        "e8": lambda: select(T.e8[:, :], T.twos[0:8, :], [[1, 144]], -15, -16, [two], [("e8", 0, 144)]),
+        "and": lambda: ts(T.ci[:, 8:16], T.ci[:, 0:8], 14, None, [AND], [("ci", 0, 8)], [cb]),
+        "zc": lambda: ts(zc, T.ci[:, 14:15], 8.0, -BIG, [LT, MUL], [cb], [zcn]),
+        "oh": lambda: ts(T.oh[:, :], T.ci[:, 8:16], 0.0, 0.5, [EQ, MUL], [cb], [ohn]),
+        "g2": lambda: ts(T.g2[:, 0:1], T.ci[:, 0:1], 2040.5, None, [ADD], [("ci", 0, 8)], [("g2", 0, 1)]),
+        "m2": lambda: ts(T.m2[:, :], T.ramp[:, 0:8], T.oh[:, 1:2], 256.0, [MUL, MUL], [rp, ohn], [("m2", 0, 8)]),
+        "sc": lambda: V(lambda q: q.tensor_tensor(sc, T.oh[:, 4:6], T.oh[:, 6:8], ADD), [ohn], [scn]),
+        "wr": lambda: ts(wr, T.oh[:, 4:5], T.oh[:, 5:6], 0.25, [ADD, SUB], [ohn], [wrn]),
+        "nb": lambda: act(nb, T.oh[:, 2:3], -BIG, 2 * BIG, [ohn], [nbn]),
+        "kc": lambda: act(kc, T.oh[:, 2:3], 0.0, float(OWN), [ohn], [kcn]),
+        "bi": lambda: act(bi, sc, nb, 2 * BIG, [scn, nbn], [bin_]),
+        "gcol": lambda: act(gcol, T.g2[:, 0:1], -2048.0, 1.0, [("g2", 0, 1)], [gcn]),
+        "dh": lambda: ts(T.dp[0:16, 0:128], T.dd[:, :], -4.0, 0.0, [ADD, MAX], [("dd", 0, 128)], [dp]),
+        "dl": lambda: V(lambda q: q.tensor_tensor(T.dp[32:48, 0:128], T.dd[:, :], T.dp[0:16, 0:128], SUB),
+                        [("dd", 0, 128), dp], [dp]),
+        "dist": lambda: op("p", dist, [("wd", 0, 144), dp], [("pv", 0, NT + 2)]),
+        "vals": values,
+        "x1": lambda: ts(T.x1[:, :], T.x[:, :], 1.0, None, [ADD], [("x", 0, NT)], [("x1", 0, NT)]),
+        "sums": lambda: V(lambda q: q.tensor_tensor_scan(T.xi[:, :], T.x1[:, :], T.ones[0:8, 0:NT], -1.0, ADD, MUL),
+                          [one, ("x1", 0, NT)], [("xi", 0, NT)]),
+        "ends": lambda: op("p", ends, [("e8", 0, 144), ("xi", 0, NT)], [("psx", 0, 16)]),
+        "el": lambda: ts(T.el[:, :], T.psx[:, 0:16], 0.5, None, [MUL], [("psx", 0, 16)], [("el", 0, 16)]),
+        "ee": lambda: ts(T.ee[:, :], T.ramp[:, 1:145], gcol, wr, [EQ, MUL], [rp, gcn, wrn], [("ee", 0, 144)]),
+        "r0": lambda: ramp_block(0), "r1": lambda: ramp_block(1),
+        "copy": lambda: dma("y", "dw", T.w1[:, 0:1024], T.w0[:, 0:1024], [("w0", 0, 1024)], [("w1", 0, 1024)]),
+    }
+    for name in (ORDER if rank else ORDER0).split():
+        if name in steps:
+            steps[name]()
+        elif name[0] == "z":
+            fill(name[1], int(name[2]))
+        else:
+            shifted(name[0], int(name[1]), 512 * "abcd".index(name[2]))
 
-    V(lambda q: q.tensor_copy(z(0, P).indirect(T.sl[:, 0:16]), T.vals[:, :]), [("sl", 0, 16), ("vals", 0, NT)], [zt(0, P)])
-    ts(T.ee[:, :], T.ramp[:, 0:144], T.e15[:, 0:1], T.wr[:, 0:1], [EQ, MUL], [rp, ("e15", 0, 1), ("wr", 0, 1)],
-       [("ee", 0, 144)])
-    V(lambda q: q.tensor_copy(z(0, P).indirect(T.el[:, 0:16]), T.vend[:, :]), [("el", 0, 16), ("vend", 0, NT)], [zt(0, P)])
+    V(lambda q: q.tensor_copy(z(0, P).indirect(T.el[:, 0:16]), T.vals[:, :]), [("el", 0, 16), ("vals", 0, 2)], [zt(0, P)])
 
-    def pointers(h):
-        lo, hi = H * h, H * h + H
-        if h:
+    def pointers(lo, hi):
+        if lo:
             ini, r = T.w0[:, OWN + lo - 1:OWN + lo], ("w0", OWN + lo - 1, OWN + lo)
         else:
-            ini, r = T.k11[:, 0:1], ("k11", 0, 1)
-        V(lambda q: q.tensor_tensor_scan(T.w0[:, OWN + lo:OWN + hi], z(lo, hi), T.w0[:, lo:hi], ini, ADD, MAX),
-          [zt(lo, hi), ("w0", lo, hi), r], [("w0", OWN + lo, OWN + hi)])
+            ini, r = T.ini[:, 0:1], ("ini", 0, 1)
+        V(lambda q: q.tensor_tensor_scan(T.w0[:, OWN + lo:OWN + hi], z(lo, hi), fix[0][:, lo:hi], ini, ADD, MAX),
+          [zt(lo, hi), (fixn[0], lo, hi), r], [("w0", OWN + lo, OWN + hi)])
 
     sent = [0]
 
@@ -266,21 +277,6 @@ def rank_program(g, core, T, topo):
             g.remote_dma(out_ap=out, in_ap=in_, remote_sem=T.sem[sem], local_sem=T.sem.sent, pid=pid, routing_id=rid,
                          dma_engine_mask=topo.mask(core, cores[r]))
             sent[0] += len(topo.engines(core, cores[r]))
-    if later:
-        ready("g", [("w0", 0, COPIED)], [])
-    for r in later:
-        send([r], T["tk%d" % rank][:, :], T["tk%d" % rank][:, :], "rle%d" % rank, [("tk%d" % rank, 0, NT)])
-        send([r], T["er%d" % rank][:, :], T.el[:, :], "re%d" % rank, [("el", 0, 16)])
-
-    def blank():
-        for k, lo in enumerate([H] + ([OWN, OWN + H] if rank else [])):
-            dma("y", "dz%d" % k, tb[0][:, lo:lo + H], tb[0][:, 0:H], [("tb0", 0, H)], [("tb0", lo, lo + H)])
-    for s in range(rank - 1, 0, -1):
-        iota(tb[s][:, OWN:WIN], [[0, P]], 0, 0, [(tbn[s], OWN, WIN)])
-    if not later:
-        blank()
-
-    pc, pcn = [T.pc0, T.pc1], ["pc0", "pc1"]
 
     def letters(k):
         for s, lo, hi in LETTERS[rank].get(k, []):
@@ -288,64 +284,81 @@ def rank_program(g, core, T, topo):
             V(lambda q: q.tensor_copy(tb[s][:, OWN:WIN].indirect(T[name][:, lo // 16:hi // 16]), src[:, lo:hi]),
               [(name, 0, 16), ("tk%d" % s, lo, hi)], [(tbn[s], OWN, WIN)])
 
-    def spread(k, h):
-        lo = OWN + H * h
+    def spread(k, b):
+        lo, hi = BLOCKS[b]
 
         def call(q):
             for j in range(16):
-                i = q.matmul(pc[h][:, 0:64], T.ee[:, 15 - j:143 - j], w[k][:, lo + j:lo + H:16], j == 0, j == 15)
+                i = q.matmul(T["pc%d" % b][:, 0:(hi - lo) // 16], T.ee[:, 15 - j:143 - j],
+                             w[k][:, OWN + lo + j:OWN + hi:16], j == 0, j == 15)
             return i
-        op("p", call, [(wn[k], lo, lo + H), ("ee", 0, 144)], [(pcn[h], 0, 64)])
+        op("p", call, [(wn[k], OWN + lo, OWN + hi), ("ee", 0, 144)], [("pc%d" % b, 0, 1)])
 
-    def listed(h):
-        V(lambda q: q.tensor_copy(T.ll[:, 64 * h:64 * h + 64], pc[h][:, 0:64]), [(pcn[h], 0, 64)], [("ll", 64 * h, 64 * h + 64)])
+    def listed(b, base=0):
+        lo, hi = BLOCKS[b]
+        ts(T.ll[:, lo // 16:hi // 16], T["pc%d" % b][:, 0:(hi - lo) // 16], -4.0, float(-base), [MUL, ADD],
+           [("pc%d" % b, 0, 1)], [("ll", lo // 16, hi // 16)])
 
-    def gather(e, out, outn, off, win, winn, top, lst, lstn, lo, hi):
-        o, src = out[:, off + lo:off + hi], win[:, 0:top].indirect(lst[:, lo // 16:hi // 16])
-        rd, wr = [(winn, 0, top), (lstn, lo // 16, hi // 16)], [(outn, off + lo, off + hi)]
+    def gather(e, out, outn, off, win, winn, base, top, lst, lstn, lo, hi):
+        o, src = out[:, off + lo:off + hi], win[:, base:top].indirect(lst[:, lo // 16:hi // 16])
+        rd, wr = [(winn, base, top), (lstn, lo // 16, hi // 16)], [(outn, off + lo, off + hi)]
         if e == "v":
             V(lambda q: q.tensor_copy(o, src), rd, wr)
         else:
             op("s", lambda q: q.activation(o, src, AF.Copy), rd, wr)
-    pointers(0)
+    pointers(*BLOCKS[0])
     spread(0, 0)
-    pointers(1)
-    spread(0, 1)
-    for r in range(ROUNDS):
-        a, b = r % 2, (r + 1) % 2
-        for h in range(2):
-            lo, k = H * h, 2 * r + h
-            top = OWN + lo + H
-            mid = lo + (CUT if k in LETTERS[rank] else SPLIT)
-            listed(h)
-            gather("s", w[b], wn[b], OWN, w[a], wn[a], top, T.ll, "ll", mid, lo + H)
-            gather("v", w[b], wn[b], OWN, w[a], wn[a], top, T.ll, "ll", lo, mid)
-            spread(b, h)
-            letters(k)
-            if k == BLANK and later:
-                ready("y", [(wn[b], OWN + lo, OWN + mid)], [])
-                blank()
-    listed(0)
-    if rank == 0:
-        send([end], T.lr0[:, 0:64], T.ll[:, 0:64], "rl0", [("ll", 0, 64)])
-    letters("a")
-    listed(1)
-    if rank == 0:
-        send([end], T.lr0[:, 64:128], T.ll[:, 64:128], "rlb", [("ll", 64, 128)])
-        send(later[1:], T.lr0[:, :], T.ll[:, :], "rl0", [("ll", 0, 128)])
-    elif later:
-        send(later, T["lr%d" % rank][:, :], T.ll[:, :], "rl%d" % rank, [("ll", 0, 128)])
+    pointers(BLOCKS[1][0], P)
+    for b in range(1, len(BLOCKS)):
+        spread(0, b)
 
-    letters("b")
+    if rank == 0:
+        for k in range(2):
+            iota(w[k][:, FIRST:OWN], [[0, OWN - FIRST]], 0, 0, [(wn[k], FIRST, OWN)])
+    elif later:
+        ready("g", [("w0", 0, 1536)], [])
+    for r in later:
+        send([r], T["tk%d" % rank][:, :], T["tk%d" % rank][:, :], "rle%d" % rank, [("tk%d" % rank, 0, NT)])
+        send([r], T["er%d" % rank][:, :], T.el[:, :], "re%d" % rank, [("el", 0, 16)])
+    if tbn[0] == "tb0":
+        iota(tb[0][:, FIRST:OWN], [[0, OWN - FIRST]], 0, 0, [(tbn[0], FIRST, OWN)])
+    if not later:
+        for s in range(rank - 1, 0, -1):
+            iota(tb[s][:, OWN:WIN], [[0, P]], 0, 0, [(tbn[s], OWN, WIN)])
+        dma("y", "dz", tb[0][:, OWN:WIN], T.w0[:, 0:OWN], [("w0", 0, OWN)], [(tbn[0], OWN, WIN)])
+
+    for r in range(ROUNDS):
+        a, c = r % 2, (r + 1) % 2
+        for b, (lo, hi) in enumerate(BLOCKS):
+            k = len(BLOCKS) * r + b
+            mid = lo + (CUT if k in LETTERS[rank] else SPLIT if rank else SPLIT0)
+            listed(b, base[rank])
+            letters(k)
+            for e, d0, d1 in (("s", mid, hi), ("v", lo, mid)):
+                gather(e, w[c], wn[c], OWN, w[a], wn[a], base[rank], OWN + hi, T.ll, "ll", d0, d1)
+            spread(c, b)
+    if tbn[0] != "tb0":
+        act(tb[0][:, FIRST:OWN], T.ones[:, 0:OWN - FIRST], 0.0, 0.0, [one], [(tbn[0], FIRST, OWN)])
+    for b, (lo, hi) in enumerate(BLOCKS):
+        listed(b, base[rank])
+        if rank == 0:
+            send([r for r in later if r in BYBLOCK], T.lr0[:, lo // 16:hi // 16], T.ll[:, lo // 16:hi // 16], "rb%d" % b,
+                 [("ll", lo // 16, hi // 16)])
+        letters("l%d" % b)
+    if later:
+        send([r for r in later if rank or r not in BYBLOCK], T["lr%d" % rank][:, :], T.ll[:, :], "rl%d" % rank,
+             [("ll", 0, 128)])
+
     for s in range(rank):
-        n = H if halves and s == 0 else P
-        for lo in range(0, P, n):
-            for e, d in (("v", 0), ("s", n // 2)):
-                gather(e, tb[s + 1], tbn[s + 1], 0, tb[s], tbn[s], WIN, T["lr%d" % s], "lr%d" % s, lo + d, lo + d + n // 2)
-    for k, (lo, n) in enumerate(((0, 1024), (1024, 512), (1536, 512))):
+        letters("u%d" % s)
+        for lo, hi in BLOCKS if rank in BYBLOCK and s == 0 else [(0, P)]:
+            mid = lo + (hi - lo) // 64 * 32
+            for e, d0, d1 in (("v", lo, mid), ("s", mid, hi)):
+                gather(e, tb[s + 1], tbn[s + 1], 0, tb[s], tbn[s], base[s], WIN, T["lr%d" % s], "lr%d" % s, d0, d1)
+    for k, (lo, n, by) in enumerate(STORES):
         for e, d in (("v", 0), ("s", n // 2)):
-            gather(e, T.yo, "yo", 0, tb[rank], tbn[rank], WIN, T.ll, "ll", lo + d, lo + d + n // 2)
-        dma("y", "dy%d" % k, T.y[:, lo:lo + n], T.yo[:, lo:lo + n], [("yo", lo, lo + n)], [("y", lo, lo + n)])
+            gather(e, T.yo, "yo", 0, tb[rank], tbn[rank], base[rank], WIN, T.ll, "ll", lo + d, lo + d + n // 2)
+        dma(by, "dy%d" % k, T.y[:, lo:lo + n], T.yo[:, lo:lo + n], [("yo", lo, lo + n)], [("y", lo, lo + n)])
     if later:
         g.wait_ge(T.sem.sent, sent[0])
     finish("y")

from concourse.mybir import AluOpType, ActivationFunctionType

P, NT = 2048, 256
OWN = P
WIN = OWN + P
ROUNDS = 5
BIG = 4096.0
FIRST = OWN - 16
BLOCKS = ((0, 1024), (1024, 2048))
SPLIT = 480
STORES = ((0, 512, "y"), (512, 1024, "y"), (1536, 512, "s"))
LETTERS = {0: {"l1": [(0, 0, 256)]},
           1: {"l1": [(0, 0, 256), (1, 0, 256)]},
           2: {"l0": [(2, 0, 256)], "l1": [(0, 0, 256), (1, 0, 256)]},
           3: {0: [(3, 0, 96)], 1: [(3, 96, 192)], 2: [(3, 192, 256)], 5: [(0, 0, 96)], 6: [(0, 96, 192)],
               7: [(0, 192, 256)], 8: [(1, 0, 96)], 9: [(1, 96, 192)], "l0": [(1, 192, 256), (2, 0, 160)],
               "l1": [(2, 160, 256)]}}
CUT = 384
BYBLOCK = (3,)
ORDER = ("ci ones and ramp twos zc oh zs0 g2 dp0 wd nb sc gcol m2 dh kc e8 bi x1 dl zs1 sums zv3 wr dist r0 r1 ends zv2 "
         "vals s0b copy s0c s0d s1c s1d ee el")
ORDER0 = ("ci ones and ramp twos zc oh zs0 g2 dp0 wd nb sc gcol m2 dh kc e8 bi x1 dl zs1 sums zv3 wr dist r0 r1 ends zv2 "
          "vals s0b s0c s0d ee el")
SPLIT0 = 512

SCRATCH = {
    "w0": ("sbuf", [128, WIN], "bfloat16"), "w1": ("sbuf", [128, WIN], "bfloat16"),
    "tb0": ("sbuf", [128, WIN], "bfloat16"), "tb1": ("sbuf", [128, WIN], "bfloat16"),
    "tb2": ("sbuf", [128, WIN], "bfloat16"), "tb3": ("sbuf", [128, WIN], "bfloat16"),
    "tk0": ("sbuf", [128, NT], "bfloat16"), "tk1": ("sbuf", [128, NT], "bfloat16"),
    "tk2": ("sbuf", [128, NT], "bfloat16"), "tk3": ("sbuf", [128, NT], "bfloat16"),
    "yo": ("sbuf", [128, P], "bfloat16"),
    "ll": ("sbuf", [128, 128], "uint16"), "el": ("sbuf", [128, 16], "uint16"),
    "lr0": ("sbuf", [128, 128], "uint16"), "lr1": ("sbuf", [128, 128], "uint16"), "lr2": ("sbuf", [128, 128], "uint16"),
    "er0": ("sbuf", [128, 16], "uint16"), "er1": ("sbuf", [128, 16], "uint16"), "er2": ("sbuf", [128, 16], "uint16"),
    "vals": ("sbuf", [128, NT], "bfloat16"), "ini": ("sbuf", [128, 2], "bfloat16"),
    "x": ("sbuf", [8, NT], "int32"), "x1": ("sbuf", [8, NT], "float16"), "xi": ("sbuf", [8, NT], "float16"),
    "dd": ("sbuf", [16, 128], "int32"), "dp": ("sbuf", [48, 130], "bfloat16"), "wd": ("sbuf", [48, 144], "bfloat16"),
    "e8": ("sbuf", [8, 144], "float16"), "ee": ("sbuf", [128, 144], "bfloat16"),
    "ci": ("sbuf", [128, 16], "int32"), "g2": ("sbuf", [128, 2], "bfloat16"), "cc": ("sbuf", [128, 16], "bfloat16"),
    "oh": ("sbuf", [128, 8], "bfloat16"), "m2": ("sbuf", [128, 8], "bfloat16"), "sc": ("sbuf", [128, 2], "float32"),
    "ramp": ("sbuf", [128, NT], "bfloat16"), "ones": ("sbuf", [128, 512], "bfloat16"),
    "twos": ("sbuf", [48, 144], "bfloat16"),
    "pc0": ("psum", [128, 512], "float32"), "pc1": ("psum", [128, 512], "float32"), "pc2": ("psum", [128, 512], "float32"),
    "pv": ("psum", [128, 512], "float32"), "psx": ("psum", [128, 512], "float32"),
}
SEMAPHORES = (["qv", "qs", "qp", "qg", "dln", "dds", "dle", "dz", "dw", "sent"]
              + ["dy%d" % k for k in range(len(STORES))]
              + ["rle%d" % s for s in range(3)] + ["re%d" % s for s in range(3)]
              + ["rl%d" % s for s in range(3)] + ["rb%d" % b for b in range(len(BLOCKS))])

ADD, SUB, MUL, MAX = AluOpType.add, AluOpType.subtract, AluOpType.mult, AluOpType.max
EQ, LT, AND = AluOpType.is_equal, AluOpType.is_lt, AluOpType.bitwise_and
AF = ActivationFunctionType


def make_tracker(g, T):
    queues = {"v": g.vector, "s": g.scalar, "p": g.tensor, "g": g, "y": g.sync}
    known = {e: {} for e in queues}
    count, clocks, hist = {}, {}, {}

    def record(stream, value, clock, reads, writes):
        clocks[(stream, value)] = clock
        for (b, lo, hi) in writes:
            hist[b] = [h for h in hist.get(b, []) if not (lo <= h[0] and h[1] <= hi)]
            hist[b].append((lo, hi, True, stream, value))
        for (b, lo, hi) in reads:
            hist.setdefault(b, []).append((lo, hi, False, stream, value))

    def wait(e, stream, value):
        if known[e].get(stream, 0) >= value:
            return
        queues[e].wait_ge(T.sem[stream], value)
        known[e][stream] = value
        for k, n in clocks.get((stream, value), {}).items():
            if known[e].get(k, 0) < n:
                known[e][k] = n

    def ready(e, reads, writes):
        need = {}
        for group, w in ((reads, False), (writes, True)):
            for (b, lo, hi) in group:
                for h in hist.get(b, []):
                    if h[0] < hi and lo < h[1] and (h[2] or w):
                        need[h[3]] = max(need.get(h[3], 0), h[4])
        for s, n in sorted(need.items(), key=lambda x: -sum(clocks.get(x, {}).values())):
            wait(e, s, n)

    def op(e, call, reads, writes, stream=None, unit=1):
        stream = stream or "q" + e
        ready(e, reads, writes)
        inst = call(queues[e])
        inst.then_inc(T.sem[stream], unit)
        n = count.get(stream, 0) + unit
        count[stream] = n
        clock = dict(known[e])
        clock[stream] = n
        record(stream, n, clock, reads, writes)

    def arrives(stream, n, b, lo, hi):
        count[stream] = n
        record(stream, n, {stream: n}, [], [(b, lo, hi)])

    def finish(e):
        for s, n in count.items():
            wait(e, s, n)

    return op, ready, arrives, finish


def rank_program(g, core, T, topo):
    rank = T.rank_of(core)
    if rank is None:
        return
    cores = T.cores
    end = len(cores) - 1
    later = list(range(end, rank, -1))
    op, ready, arrives, finish = make_tracker(g, T)
    w = [T.w0, T.w1]
    wn = ["w0", "w1"]
    tbn = ["tb%d" % s if s == rank or not later else wn[s] for s in range(rank + 1)]
    tb = [T[n] for n in tbn]

    def V(call, reads, writes):
        op("v", call, reads, writes)

    def ts(out, in0, s1, s2, ops, reads, writes):
        if s2 is None:
            V(lambda q: q.tensor_scalar(out, in0, s1, None, ops[0]), reads, writes)
        else:
            V(lambda q: q.tensor_scalar(out, in0, s1, s2, ops[0], ops[1]), reads, writes)

    def act(out, in_, bias, scale, reads, writes):
        op("s", lambda q: q.activation(out, in_, AF.Identity, bias=bias, scale=scale), reads, writes)

    def dma(e, stream, out, in_, reads, writes):
        op(e, lambda q: q.dma_start(out, in_), reads, writes, stream, 16)

    def iota(out, pattern, base, cm, writes, flag=True):
        if flag:
            op("g", lambda q: q.iota(out, pattern, base, cm, allow_small_or_imprecise_dtypes=True), [], writes)
        else:
            op("g", lambda q: q.iota(out, pattern, base, cm), [], writes)

    def select(out, in_, pattern, base, cm, reads, writes):
        op("g", lambda q: q.affine_select(out, in_, pattern, EQ, 0.0, base, cm), reads, writes)

    def z(lo, hi):
        return tb[rank][:, OWN + lo:OWN + hi]

    def zt(lo, hi):
        return (tbn[rank], OWN + lo, OWN + hi)

    for s in range(rank):
        n = len(topo.engines(cores[s], core))
        arrives("rle%d" % s, n, "tk%d" % s, 0, NT)
        arrives("re%d" % s, n, "er%d" % s, 0, 16)
        if rank in BYBLOCK and s == 0:
            for b, (lo, hi) in enumerate(BLOCKS):
                arrives("rb%d" % b, n, "lr0", lo // 16, hi // 16)
        else:
            arrives("rl%d" % s, n, "lr%d" % s, 0, 128)

    dma("s", "dds", T.dd[:, :], T.ds[:, :], [], [("dd", 0, 128)])
    dma("y", "dln", T.x[:, :], T.ln[:, :], [], [("x", 0, NT)])
    dma("y", "dle", T["tk%d" % rank][:, :], T.le[:, :], [], [("tk%d" % rank, 0, NT)])

    def column(k, n=1):
        return T.cc[:, k:k + n], ("cc", k, k + n)
    zc, zcn = column(0)
    wr, wrn = column(1)
    sc, scn = T.sc[:, :], ("sc", 0, 2)
    nb, nbn = column(4)
    kc, kcn = column(5)
    bi, bin_ = column(6, 2)
    gcol, gcn = column(8)
    one, rp, dp, cb, ohn = ("ones", 0, 512), ("ramp", 0, NT), ("dp", 0, 130), ("ci", 8, 16), ("oh", 0, 8)
    two = ("twos", 0, 144)

    def fill(e, k):
        lo, hi = 512 * k, 512 * k + 512
        if e == "s":
            act(z(lo, hi), T.ones[:, :], zc, 0.0, [one, zcn], [zt(lo, hi)])
        elif e == "v":
            ts(z(lo, hi), T.ones[:, :], zc, None, [MUL], [one, zcn], [zt(lo, hi)])
        else:
            select(z(lo, hi), z(0, 512), [[0, 512]], 0, 0, [zt(0, 512)], [zt(lo, hi)])

    fixn = wn if rank else ["yo"]
    fix = [T[n] for n in fixn]
    base = [FIRST] + [0] * end

    def ramp_block(b):
        ts(fix[0][:, 256 * b:256 * b + 256], T.ramp[:, :], T.oh[:, 0:1], T.m2[:, b:b + 1], [MUL, ADD],
           [rp, ohn, ("m2", 0, 8)], [(fixn[0], 256 * b, 256 * b + 256)])

    def shifted(e, k, lo):
        rd, wt, c = [(fixn[0], 0, 512), ("m2", 0, 8)], [(fixn[k], lo, lo + 512)], T.m2[:, lo // 256:lo // 256 + 1]
        if e == "s":
            act(fix[k][:, lo:lo + 512], fix[0][:, 0:512], c, 1.0, rd, wt)
        else:
            ts(fix[k][:, lo:lo + 512], fix[0][:, 0:512], c, None, [ADD], rd, wt)

    def dist(q):
        q.matmul(T.pv[:, 0:128], T.wd[:, 8:136], T.dp[:, 0:128], True, True)
        return q.matmul(T.pv[:, 128:NT + 2], T.wd[:, 16:144], T.dp[:, :], True, True)

    def ends(q):
        for j in range(16):
            i = q.matmul(T.psx[:, 0:16], T.e8[:, 15 - j:143 - j], T.xi[:, j:NT:16], j == 0, j == 15)
        return i

    def values():
        for par in range(2):
            c = 1 - par
            act(T.vals[:, par:NT:2], T.pv[:, par + 1:NT + 1:2], T.cc[:, 6 + c:7 + c], T.sc[:, c:c + 1],
                [("pv", 0, NT + 2), scn, bin_], [("vals", par, par + 1)])
        act(T.ini[:, 0:1], T.pv[:, 0:1], kc, T.sc[:, 0:1], [("pv", 0, NT + 2), scn, kcn], [("ini", 0, 1)])
    steps = {
        "ones": lambda: V(lambda q: q.memset(T.ones[:, :], 1.0), [], [one]),
        "twos": lambda: iota(T.twos[:, :], [[0, 144]], 2, 0, [two]),
        "dp0": lambda: V(lambda q: q.memset(T.dp[:, :], 0.0), [], [dp]),
        "ramp": lambda: V(lambda q: q.tensor_tensor_scan(T.ramp[:, :], T.ones[:, 0:NT], T.ones[:, 0:NT], -1.0, ADD, MUL),
                          [one], [rp]),
        "ci": lambda: iota(T.ci[:, 0:8], [[-2, 8]], 16, 1, [("ci", 0, 8)], False),
        "wd": lambda: select(T.wd[:, :], T.twos[:, :], [[1, 18], [0, 4], [32, 2]], -2, -1, [two], [("wd", 0, 144)]),
        "e8": lambda: select(T.e8[:, :], T.twos[0:8, :], [[1, 144]], -15, -16, [two], [("e8", 0, 144)]),
        "and": lambda: ts(T.ci[:, 8:16], T.ci[:, 0:8], 14, None, [AND], [("ci", 0, 8)], [cb]),
        "zc": lambda: ts(zc, T.ci[:, 14:15], 8.0, -BIG, [LT, MUL], [cb], [zcn]),
        "oh": lambda: ts(T.oh[:, :], T.ci[:, 8:16], 0.0, 0.5, [EQ, MUL], [cb], [ohn]),
        "g2": lambda: ts(T.g2[:, 0:1], T.ci[:, 0:1], 2040.5, None, [ADD], [("ci", 0, 8)], [("g2", 0, 1)]),
        "m2": lambda: ts(T.m2[:, :], T.ramp[:, 0:8], T.oh[:, 1:2], 256.0, [MUL, MUL], [rp, ohn], [("m2", 0, 8)]),
        "sc": lambda: V(lambda q: q.tensor_tensor(sc, T.oh[:, 4:6], T.oh[:, 6:8], ADD), [ohn], [scn]),
        "wr": lambda: ts(wr, T.oh[:, 4:5], T.oh[:, 5:6], 0.25, [ADD, SUB], [ohn], [wrn]),
        "nb": lambda: act(nb, T.oh[:, 2:3], -BIG, 2 * BIG, [ohn], [nbn]),
        "kc": lambda: act(kc, T.oh[:, 2:3], 0.0, float(OWN), [ohn], [kcn]),
        "bi": lambda: act(bi, sc, nb, 2 * BIG, [scn, nbn], [bin_]),
        "gcol": lambda: act(gcol, T.g2[:, 0:1], -2048.0, 1.0, [("g2", 0, 1)], [gcn]),
        "dh": lambda: ts(T.dp[0:16, 0:128], T.dd[:, :], -4.0, 0.0, [ADD, MAX], [("dd", 0, 128)], [dp]),
        "dl": lambda: V(lambda q: q.tensor_tensor(T.dp[32:48, 0:128], T.dd[:, :], T.dp[0:16, 0:128], SUB),
                        [("dd", 0, 128), dp], [dp]),
        "dist": lambda: op("p", dist, [("wd", 0, 144), dp], [("pv", 0, NT + 2)]),
        "vals": values,
        "x1": lambda: ts(T.x1[:, :], T.x[:, :], 1.0, None, [ADD], [("x", 0, NT)], [("x1", 0, NT)]),
        "sums": lambda: V(lambda q: q.tensor_tensor_scan(T.xi[:, :], T.x1[:, :], T.ones[0:8, 0:NT], -1.0, ADD, MUL),
                          [one, ("x1", 0, NT)], [("xi", 0, NT)]),
        "ends": lambda: op("p", ends, [("e8", 0, 144), ("xi", 0, NT)], [("psx", 0, 16)]),
        "el": lambda: ts(T.el[:, :], T.psx[:, 0:16], 0.5, None, [MUL], [("psx", 0, 16)], [("el", 0, 16)]),
        "ee": lambda: ts(T.ee[:, :], T.ramp[:, 1:145], gcol, wr, [EQ, MUL], [rp, gcn, wrn], [("ee", 0, 144)]),
        "r0": lambda: ramp_block(0), "r1": lambda: ramp_block(1),
        "copy": lambda: dma("y", "dw", T.w1[:, 0:1024], T.w0[:, 0:1024], [("w0", 0, 1024)], [("w1", 0, 1024)]),
    }
    for name in (ORDER if rank else ORDER0).split():
        if name in steps:
            steps[name]()
        elif name[0] == "z":
            fill(name[1], int(name[2]))
        else:
            shifted(name[0], int(name[1]), 512 * "abcd".index(name[2]))

    V(lambda q: q.tensor_copy(z(0, P).indirect(T.el[:, 0:16]), T.vals[:, :]), [("el", 0, 16), ("vals", 0, 2)], [zt(0, P)])

    def pointers(lo, hi):
        if lo:
            ini, r = T.w0[:, OWN + lo - 1:OWN + lo], ("w0", OWN + lo - 1, OWN + lo)
        else:
            ini, r = T.ini[:, 0:1], ("ini", 0, 1)
        V(lambda q: q.tensor_tensor_scan(T.w0[:, OWN + lo:OWN + hi], z(lo, hi), fix[0][:, lo:hi], ini, ADD, MAX),
          [zt(lo, hi), (fixn[0], lo, hi), r], [("w0", OWN + lo, OWN + hi)])

    sent = [0]

    def send(to, out, in_, sem, reads):
        ready("g", reads, [])
        for r in to:
            rid, pid = topo.addr(cores[r])[:2]
            g.remote_dma(out_ap=out, in_ap=in_, remote_sem=T.sem[sem], local_sem=T.sem.sent, pid=pid, routing_id=rid,
                         dma_engine_mask=topo.mask(core, cores[r]))
            sent[0] += len(topo.engines(core, cores[r]))

    def letters(k):
        for s, lo, hi in LETTERS[rank].get(k, []):
            name, src = "er%d" % s if s < rank else "el", T["tk%d" % s]
            V(lambda q: q.tensor_copy(tb[s][:, OWN:WIN].indirect(T[name][:, lo // 16:hi // 16]), src[:, lo:hi]),
              [(name, 0, 16), ("tk%d" % s, lo, hi)], [(tbn[s], OWN, WIN)])

    def spread(k, b):
        lo, hi = BLOCKS[b]

        def call(q):
            for j in range(16):
                i = q.matmul(T["pc%d" % b][:, 0:(hi - lo) // 16], T.ee[:, 15 - j:143 - j],
                             w[k][:, OWN + lo + j:OWN + hi:16], j == 0, j == 15)
            return i
        op("p", call, [(wn[k], OWN + lo, OWN + hi), ("ee", 0, 144)], [("pc%d" % b, 0, 1)])

    def listed(b, base=0):
        lo, hi = BLOCKS[b]
        ts(T.ll[:, lo // 16:hi // 16], T["pc%d" % b][:, 0:(hi - lo) // 16], -4.0, float(-base), [MUL, ADD],
           [("pc%d" % b, 0, 1)], [("ll", lo // 16, hi // 16)])

    def gather(e, out, outn, off, win, winn, base, top, lst, lstn, lo, hi):
        o, src = out[:, off + lo:off + hi], win[:, base:top].indirect(lst[:, lo // 16:hi // 16])
        rd, wr = [(winn, base, top), (lstn, lo // 16, hi // 16)], [(outn, off + lo, off + hi)]
        if e == "v":
            V(lambda q: q.tensor_copy(o, src), rd, wr)
        else:
            op("s", lambda q: q.activation(o, src, AF.Copy), rd, wr)
    pointers(*BLOCKS[0])
    spread(0, 0)
    pointers(BLOCKS[1][0], P)
    for b in range(1, len(BLOCKS)):
        spread(0, b)

    if rank == 0:
        for k in range(2):
            iota(w[k][:, FIRST:OWN], [[0, OWN - FIRST]], 0, 0, [(wn[k], FIRST, OWN)])
    elif later:
        ready("g", [("w0", 0, 1536)], [])
    for r in later:
        send([r], T["tk%d" % rank][:, :], T["tk%d" % rank][:, :], "rle%d" % rank, [("tk%d" % rank, 0, NT)])
        send([r], T["er%d" % rank][:, :], T.el[:, :], "re%d" % rank, [("el", 0, 16)])
    if tbn[0] == "tb0":
        iota(tb[0][:, FIRST:OWN], [[0, OWN - FIRST]], 0, 0, [(tbn[0], FIRST, OWN)])
    if not later:
        for s in range(rank - 1, 0, -1):
            iota(tb[s][:, OWN:WIN], [[0, P]], 0, 0, [(tbn[s], OWN, WIN)])
        dma("y", "dz", tb[0][:, OWN:WIN], T.w0[:, 0:OWN], [("w0", 0, OWN)], [(tbn[0], OWN, WIN)])

    for r in range(ROUNDS):
        a, c = r % 2, (r + 1) % 2
        for b, (lo, hi) in enumerate(BLOCKS):
            k = len(BLOCKS) * r + b
            mid = lo + (CUT if k in LETTERS[rank] else SPLIT if rank else SPLIT0)
            listed(b, base[rank])
            letters(k)
            for e, d0, d1 in (("s", mid, hi), ("v", lo, mid)):
                gather(e, w[c], wn[c], OWN, w[a], wn[a], base[rank], OWN + hi, T.ll, "ll", d0, d1)
            spread(c, b)
    if tbn[0] != "tb0":
        act(tb[0][:, FIRST:OWN], T.ones[:, 0:OWN - FIRST], 0.0, 0.0, [one], [(tbn[0], FIRST, OWN)])
    for b, (lo, hi) in enumerate(BLOCKS):
        listed(b, base[rank])
        if rank == 0:
            send([r for r in later if r in BYBLOCK], T.lr0[:, lo // 16:hi // 16], T.ll[:, lo // 16:hi // 16], "rb%d" % b,
                 [("ll", lo // 16, hi // 16)])
        letters("l%d" % b)
    if later:
        send([r for r in later if rank or r not in BYBLOCK], T["lr%d" % rank][:, :], T.ll[:, :], "rl%d" % rank,
             [("ll", 0, 128)])

    for s in range(rank):
        letters("u%d" % s)
        for lo, hi in BLOCKS if rank in BYBLOCK and s == 0 else [(0, P)]:
            mid = lo + (hi - lo) // 64 * 32
            for e, d0, d1 in (("v", lo, mid), ("s", mid, hi)):
                gather(e, tb[s + 1], tbn[s + 1], 0, tb[s], tbn[s], base[s], WIN, T["lr%d" % s], "lr%d" % s, d0, d1)
    for k, (lo, n, by) in enumerate(STORES):
        for e, d in (("v", 0), ("s", n // 2)):
            gather(e, T.yo, "yo", 0, tb[rank], tbn[rank], base[rank], WIN, T.ll, "ll", lo + d, lo + d + n // 2)
        dma(by, "dy%d" % k, T.y[:, lo:lo + n], T.yo[:, lo:lo + n], [("yo", lo, lo + n)], [("y", lo, lo + n)])
    if later:
        g.wait_ge(T.sem.sent, sent[0])
    finish("y")
